import numpy as np
import ml_dtypes


def mxq(x, axis, fmt="e4m3"):
    dtype, down = {"e4m3": (ml_dtypes.float8_e4m3fn, 7), "e5m2": (ml_dtypes.float8_e5m2, 14)}[fmt]
    v = np.moveaxis(np.asarray(x, np.float32).astype(ml_dtypes.bfloat16).astype(np.float64), axis, -1)
    blocks = v.reshape(v.shape[:-1] + (-1, 32))
    amax = np.abs(blocks).max(-1, keepdims=True)
    byte = np.maximum(np.where(amax > 0, np.frexp(amax)[1] - 1 + 127, 0) - down, 1)
    scale = np.exp2(byte - 127.0)
    codes = (blocks / scale).astype(np.float32).astype(dtype).astype(np.float64)
    return np.moveaxis((codes * scale).reshape(v.shape), -1, axis)


WIDE = False


def mx_kscale(k):
    if not WIDE:
        return np.ones(k)
    levels = np.array([10, -10, 5, -5, 0])
    if k % 512:
        return np.exp2(np.random.permutation(np.resize(levels, k // 32))).repeat(32)
    a = np.empty((k // 512, 16))
    for p in range(k // 512):
        a[p, :8] = np.random.permutation(np.resize(levels, 8))
        for g in range(8):
            far = levels[np.abs(levels - a[p, g]) >= 10]
            a[p, g + 8] = far[np.random.randint(len(far))]
    return np.exp2(a.ravel()).repeat(32)


def f64(x):
    return np.asarray(x).astype(np.float64)


def striped(idx):
    return np.tile(np.asarray(idx).reshape(-1, 16).T, (8, 1)).astype(np.uint16)


def unstriped(offs):
    return offs[:16].T.reshape(-1).astype(np.int64)


E2M1 = np.array([0.0, 0.5, 1.0, 1.5, 2.0, 3.0, 4.0, 6.0, -0.0, -0.5, -1.0, -1.5, -2.0, -3.0, -4.0, -6.0])


def pack_weight(w, fmt):
    k, n = w.shape
    w = f64(np.asarray(w, np.float32).astype(ml_dtypes.bfloat16)).reshape(k // 32, 32, n)
    amax = np.abs(w).max(1)
    if fmt == "e4m3":
        byte = np.frexp(amax)[1] - 1 + 127 - 7
    else:
        mant, ex = np.frexp(amax / 6.0)
        byte = np.where(mant > 0.5, ex, ex - 1) + 127
    byte = np.clip(np.where(amax > 0, byte, 1), 1, 254)
    scaled = (w * np.exp2(127.0 - byte)[:, None, :]).reshape(k, n).astype(np.float32)
    by_word = np.ascontiguousarray(scaled.reshape(k // 512, 128, 4, n).transpose(0, 1, 3, 2))
    if fmt == "e4m3":
        words = by_word.astype(ml_dtypes.float8_e4m3fn).view(np.uint8)
    else:
        c = by_word.astype(ml_dtypes.float4_e2m1fn).view(np.uint8) & 0xF
        words = (c[..., 0::2] | (c[..., 1::2] << 4)).reshape(k // 512, 128, 2 * n)
    return np.ascontiguousarray(words), np.ascontiguousarray(byte.astype(np.uint8).reshape(k // 512, 16, n))


def unpack_weight(words, scales, fmt):
    g, _, n = scales.shape
    words = np.ascontiguousarray(words).reshape(g, 128, n, -1)
    if fmt == "e4m3":
        vals = words.view(ml_dtypes.float8_e4m3fn).astype(np.float64)
    else:
        nib = np.empty((g, 128, n, 4), np.uint8)
        nib[..., 0::2] = words & 0xF
        nib[..., 1::2] = words >> 4
        vals = E2M1[nib]
    vals = vals * np.repeat(np.exp2(scales.astype(np.float64) - 127.0), 8, axis=1)[..., None]
    return vals.transpose(0, 1, 3, 2).reshape(g * 512, n)


D, E, T, I, Q = 512, 512, 2048, 512, 128


def setup_inputs():
    n = np.random.standard_normal
    idx = np.random.permutation(T)[:I]
    fd = mx_kscale(D)
    fi = mx_kscale(I)
    ti = np.ones(T)
    ti[idx] = fi
    keysp = pack_weight(n((D, T)) / fd[:, None], "e4m3")
    return {
        "query": (n((D, Q)) * 0.7 / np.sqrt(D) * fd[:, None]).astype(np.float32),
        "keys_words": keysp[0],
        "keys_scales": keysp[1],
        "dquery": (n((D, Q)) * 0.6 / np.sqrt(D) * fd[:, None]).astype(np.float32),
        "os": (np.random.uniform(0.2, 0.8, (1, I)) * fi).astype(np.float32),
        "vals": (n((E, T)) / ti).astype(np.float32),
        "offs": striped(idx),
    }


def reference(query, keys_words, keys_scales, dquery, os, vals, offs):
    idx = unstriped(offs)
    keysu = unpack_weight(keys_words, keys_scales, "e4m3")
    queryq = mxq(f64(query), 0, "e4m3")
    keysidxg = keysu[:, idx]
    a = queryq.T @ keysidxg
    dqueryq = mxq(f64(dquery), 0, "e4m3")
    ta = dqueryq.T @ keysidxg
    p = np.exp(a - np.max(a, axis=1, keepdims=True))
    n2 = np.sqrt(np.sum(np.square(p), axis=1, keepdims=True))
    tp = ta * p
    tn2 = np.sum(tp * p * 2.0, axis=1, keepdims=True) * 0.5 / n2
    tw = (tp - tn2 * p / n2) / n2
    wo1 = tw * f64(os)
    wt1 = wo1.T
    vt1 = f64(vals)[:, idx].T
    wt1q = mxq(wt1, 0, "e4m3")
    vt1q = mxq(vt1, 0, "e4m3")
    o = wt1q.T @ vt1q
    return o

@@ -1,0 +1,178 @@
+from contextlib import ExitStack
+
+import concourse.mybir as mybir
+from concourse.masks import make_identity
+
+F32 = mybir.dt.float32
+BF16 = mybir.dt.bfloat16
+I32 = mybir.dt.int32
+U32 = mybir.dt.uint32
+U16 = mybir.dt.uint16
+U8 = mybir.dt.uint8
+FP8X4 = mybir.dt.float8_e4m3fn_x4
+ALU = mybir.AluOpType
+ACT = mybir.ActivationFunctionType
+AXIS = mybir.AxisListType
+
+P = 128
+PACK = 4
+D, E, T, I, Q = 512, 512, 2048, 512, 128
+BLOCKS = E // P
+FLOPS = 2 * Q * I * (2 * D + E)
+
+
+def tile_attend_ttunitweights_kernel(tc, query, keys_words, keys_scales, dquery, slot_factor, vals, offs, out):
+    nc = tc.nc
+    with ExitStack() as ctx:
+        held = ctx.enter_context(tc.tile_pool(name="held", bufs=1))
+        psum = ctx.enter_context(tc.psum_pool(name="psum", bufs=1))
+
+        offsets = held.tile([P, I // 16], U16, name="offsets")
+        key_pool = held.tile([P, T], U32, name="key_pool", align_bytes=64)
+        scale_pool = held.tile([P, T], U8, name="scale_pool", align_bytes=64)
+        q_raw = held.tile([P, PACK, Q], F32, name="q_raw")
+        dq_raw = held.tile([P, PACK, Q], F32, name="dq_raw")
+        os_col = held.tile([P, PACK], F32, name="os_col")
+        val_pool = [held.tile([P, T], F32, name=f"val_pool{b}") for b in range(BLOCKS)]
+
+        nc.gpsimd.memset(scale_pool[:].bitcast(I32), 0)
+        nc.sync.dma_start(key_pool[:].bitcast(I32), keys_words[0].rearrange("p n t -> p (n t)").bitcast(I32))
+        nc.sync.dma_start(offsets[:], offs)
+        for quad in range(4):
+            nc.scalar.dma_start(
+                scale_pool[32 * quad : 32 * quad + 4, :].bitcast(I32),
+                keys_scales[0, 4 * quad : 4 * quad + 4, :].bitcast(I32),
+            )
+        nc.sync.dma_start(q_raw[:], query.rearrange("(p j) q -> p j q", j=PACK))
+        nc.sync.dma_start(dq_raw[:], dquery.rearrange("(p j) q -> p j q", j=PACK))
+        nc.sync.dma_start(os_col[:], slot_factor.rearrange("o (p t) -> (o p) t", t=PACK))
+        for b in range(BLOCKS):
+            nc.sync.dma_start(val_pool[b][:], vals[b * P : (b + 1) * P, :])
+
+        ident = held.tile([P, P], F32, name="ident")
+        make_identity(nc, ident[:])
+        minus_half = held.tile([P, 1], F32, name="minus_half")
+        nc.gpsimd.memset(minus_half[:], -0.5)
+        warm = held.tile([P, 1], F32, name="warm")
+        nc.scalar.activation(out=warm[:], in_=minus_half[:], func=ACT.Exp)
+
+        def quantize(name, grouped, width):
+            codes = held.tile([P, width], U32, name=name + "_codes", align_bytes=64)
+            scales = held.tile([P, width], U8, name=name + "_scales", align_bytes=64)
+            nc.vector.quantize_mx(out=codes[:].bitcast(FP8X4), scales=scales[:], in_=grouped)
+            return codes, scales
+
+        def product(result, left, right):
+            nc.tensor.matmul_mx(
+                out=result,
+                lhsT=left[0][:].bitcast(FP8X4),
+                lhsT_scale=left[1][:],
+                rhs=right[0][:].bitcast(FP8X4),
+                rhs_scale=right[1][:],
+                start=True,
+                stop=True,
+            )
+
+        def turn_pairs(name, rows, bank):
+            words = rows[:].bitcast(F32)
+            for u in range(2):
+                nc.tensor.transpose(bank[:, u, :], words[:, u : I // 2 : 2], ident[:])
+            grouped = held.tile([P, P * PACK], BF16, name=name + "_grouped", align_bytes=64)
+            nc.scalar.copy(
+                out=grouped[:].bitcast(F32).rearrange("p (c u) -> p c u", u=2),
+                in_=bank[:].rearrange("p u c -> p c u"),
+            )
+            return grouped
+
+        key_scales = held.tile([P, I], U8, name="key_scales", align_bytes=64)
+        nc.vector.tensor_copy(key_scales[:], scale_pool[:].indirect(offsets[:]))
+        key_codes = held.tile([P, I], U32, name="key_codes", align_bytes=64)
+        nc.vector.tensor_copy(key_codes[:], key_pool[:].indirect(offsets[:]))
+        keys = (key_codes, key_scales)
+
+        q_grouped = held.tile([P, Q, PACK], BF16, name="q_grouped", align_bytes=64)
+        nc.scalar.copy(out=q_grouped[:], in_=q_raw[:].rearrange("p j q -> p q j"))
+        dq_grouped = held.tile([P, Q, PACK], BF16, name="dq_grouped", align_bytes=64)
+        nc.scalar.copy(out=dq_grouped[:], in_=dq_raw[:].rearrange("p j q -> p q j"))
+        q_mx = quantize("q", q_grouped[:].rearrange("p q j -> p (q j)"), Q)
+        a = psum.tile([P, I], F32, name="a", tag="a")
+        product(a[:], q_mx, keys)
+        dq_mx = quantize("dq", dq_grouped[:].rearrange("p q j -> p (q j)"), Q)
+        ta = psum.tile([P, I], F32, name="ta")
+        product(ta[:], dq_mx, keys)
+
+        os_rows = psum.tile([P, PACK, P], F32, name="os_rows")
+        for t in range(PACK):
+            nc.tensor.transpose(os_rows[:, t, :], os_col[:, t : t + 1].to_broadcast([P, P]), ident[:])
+
+        neg_max = held.tile([P, 1], F32, name="neg_max")
+        nc.vector.tensor_reduce(out=neg_max[:], in_=a[:], axis=AXIS.X, op=ALU.max, negate=True)
+        p = held.tile([P, I], F32, name="p")
+        nc.scalar.activation(out=p[:], in_=a[:], func=ACT.Exp, bias=neg_max[:], scale=1.0)
+        p_sq = held.tile([P, I], F32, name="p_sq")
+        sum_sq = held.tile([P, 1], F32, name="sum_sq")
+        nc.scalar.activation(out=p_sq[:], in_=p[:], func=ACT.Square, accum_out=sum_sq[:])
+        inv_norm = held.tile([P, 1], F32, name="inv_norm")
+        nc.gpsimd.tensor_tensor(out=inv_norm[:], in0=sum_sq[:], in1=minus_half[:], op=ALU.pow)
+
+        val_banks = [psum.tile([P, 2, P], F32, name=f"val_bank{k}") for k in range(2)]
+        val_mx = []
+
+        def gather_values(b):
+            picked = held.tile([P, I], BF16, name=f"picked{b}", align_bytes=64)
+            nc.vector.tensor_copy(picked[:], val_pool[b][:].indirect(offsets[:]))
+            return turn_pairs(f"val{b}", picked, val_banks[b % 2])
+
+        grouped0 = gather_values(0)
+
+        ta_p_sq = held.tile([P, I], F32, name="ta_p_sq")
+        sum_cross = held.tile([P, 1], F32, name="sum_cross")
+        nc.vector.scalar_tensor_tensor(
+            out=ta_p_sq[:], in0=ta[:], scalar=1.0, in1=p_sq[:], op0=ALU.mult, op1=ALU.mult, accum_out=sum_cross[:]
+        )
+        factor = held.tile([P, P, PACK], F32, name="factor")
+        nc.vector.scalar_tensor_tensor(
+            out=factor[:],
+            in0=p[:].rearrange("q (s t) -> q s t", t=PACK),
+            scalar=inv_norm[:],
+            in1=os_rows[:].rearrange("q t s -> q s t"),
+            op0=ALU.mult,
+            op1=ALU.mult,
+        )
+        shift = held.tile([P, 1], F32, name="shift")
+        nc.vector.tensor_scalar(
+            out=shift[:], in0=sum_cross[:], scalar1=inv_norm[:], scalar2=inv_norm[:], op0=ALU.mult, op1=ALU.mult
+        )
+        val_mx.append(quantize("val0", grouped0[:], P))
+        w_rows = held.tile([P, I], BF16, name="w_rows", align_bytes=64)
+        nc.vector.scalar_tensor_tensor(
+            out=w_rows[:],
+            in0=ta[:],
+            scalar=shift[:],
+            in1=factor[:].rearrange("q s t -> q (s t)"),
+            op0=ALU.subtract,
+            op1=ALU.mult,
+        )
+        w_bank = psum.tile([P, 2, P], F32, name="w_bank", tag="a")
+        w_grouped = turn_pairs("w", w_rows, w_bank)
+
+        grouped1 = gather_values(1)
+        w_mx = quantize("w", w_grouped[:], Q)
+        grouped2 = gather_values(2)
+        val_mx.append(quantize("val1", grouped1[:], P))
+
+        early = psum.tile([P, 2, P], F32, name="early")
+        for b in range(2):
+            product(early[:, b, :], w_mx, val_mx[b])
+        early_out = held.tile([P, 2, P], F32, name="early_out")
+        nc.scalar.copy(out=early_out[:], in_=early[:])
+        nc.sync.dma_start(out[:, 0 : 2 * P], early_out[:].rearrange("q b e -> q (b e)"))
+
+        grouped3 = gather_values(3)
+        for b, grouped, drain in ((2, grouped2, nc.scalar.copy), (3, grouped3, nc.vector.tensor_copy)):
+            block_mx = quantize(f"val{b}", grouped[:], P)
+            late = psum.tile([P, P], F32, name=f"late{b}")
+            product(late[:], w_mx, block_mx)
+            late_out = held.tile([P, P], F32, name=f"late_out{b}")
+            drain(out=late_out[:], in_=late[:])
+            nc.sync.dma_start(out[:, b * P : (b + 1) * P], late_out[:])

@@ -33,19 +33,21 @@ def tile_attend_ttunitweights_kernel(tc, query, keys_words, keys_scales, dquery,
         q_raw = held.tile([P, PACK, Q], F32, name="q_raw")
         dq_raw = held.tile([P, PACK, Q], F32, name="dq_raw")
         os_col = held.tile([P, PACK], F32, name="os_col")
-        val_pool = [held.tile([P, T], F32, name=f"val_pool{b}") for b in range(BLOCKS)]
+        val_pool = [held.tile([P, T], F32, name=f"val_pool{b}", tag=f"val_pool{b}", align_bytes=64) for b in range(BLOCKS)]
 
-        nc.gpsimd.memset(scale_pool[:].bitcast(I32), 0)
-        nc.sync.dma_start(key_pool[:].bitcast(I32), keys_words[0].rearrange("p n t -> p (n t)").bitcast(I32))
+        nc.vector.memset(scale_pool[:].bitcast(I32), 0)
         nc.sync.dma_start(offsets[:], offs)
+        nc.sync.dma_start(os_col[:], slot_factor.rearrange("o (p t) -> (o p) t", t=PACK))
+        key_words = keys_words[0].rearrange("p n t -> p (n t)").bitcast(I32)
+        nc.sync.dma_start(key_pool[:, 0 : T // 2].bitcast(I32), key_words[:, 0 : T // 2])
         for quad in range(4):
-            nc.scalar.dma_start(
+            nc.sync.dma_start(
                 scale_pool[32 * quad : 32 * quad + 4, :].bitcast(I32),
                 keys_scales[0, 4 * quad : 4 * quad + 4, :].bitcast(I32),
             )
+        nc.sync.dma_start(key_pool[:, T // 2 : T].bitcast(I32), key_words[:, T // 2 : T])
         nc.sync.dma_start(q_raw[:], query.rearrange("(p j) q -> p j q", j=PACK))
         nc.sync.dma_start(dq_raw[:], dquery.rearrange("(p j) q -> p j q", j=PACK))
-        nc.sync.dma_start(os_col[:], slot_factor.rearrange("o (p t) -> (o p) t", t=PACK))
         for b in range(BLOCKS):
             nc.sync.dma_start(val_pool[b][:], vals[b * P : (b + 1) * P, :])
 
@@ -56,8 +58,8 @@ def tile_attend_ttunitweights_kernel(tc, query, keys_words, keys_scales, dquery,
         warm = held.tile([P, 1], F32, name="warm")
         nc.scalar.activation(out=warm[:], in_=minus_half[:], func=ACT.Exp)
 
-        def quantize(name, grouped, width):
-            codes = held.tile([P, width], U32, name=name + "_codes", align_bytes=64)
+        def quantize(name, grouped, width, tag=None):
+            codes = held.tile([P, width], U32, name=name + "_codes", tag=tag or name + "_codes", align_bytes=64)
             scales = held.tile([P, width], U8, name=name + "_scales", align_bytes=64)
             nc.vector.quantize_mx(out=codes[:].bitcast(FP8X4), scales=scales[:], in_=grouped)
             return codes, scales
@@ -105,13 +107,22 @@ def tile_attend_ttunitweights_kernel(tc, query, keys_words, keys_scales, dquery,
         for t in range(PACK):
             nc.tensor.transpose(os_rows[:, t, :], os_col[:, t : t + 1].to_broadcast([P, P]), ident[:])
 
-        neg_max = held.tile([P, 1], F32, name="neg_max")
-        nc.vector.tensor_reduce(out=neg_max[:], in_=a[:], axis=AXIS.X, op=ALU.max, negate=True)
-        p = held.tile([P, I], F32, name="p")
-        nc.scalar.activation(out=p[:], in_=a[:], func=ACT.Exp, bias=neg_max[:], scale=1.0)
+        doubled = held.tile([P, I], F32, name="doubled")
+        neg_two_max = held.tile([P, 1], F32, name="neg_two_max")
+        nc.vector.tensor_scalar(
+            out=doubled[:], in0=a[:], scalar1=-2.0, scalar2=None, op0=ALU.mult, op1=ALU.min, accum_out=neg_two_max[:]
+        )
         p_sq = held.tile([P, I], F32, name="p_sq")
         sum_sq = held.tile([P, 1], F32, name="sum_sq")
-        nc.scalar.activation(out=p_sq[:], in_=p[:], func=ACT.Square, accum_out=sum_sq[:])
+        nc.scalar.activation(
+            out=p_sq[:], in_=doubled[:], func=ACT.Exp, bias=neg_two_max[:], scale=-1.0, accum_out=sum_sq[:]
+        )
+        neg_max = held.tile([P, 1], F32, name="neg_max")
+        nc.gpsimd.tensor_scalar(
+            out=neg_max[:], in0=neg_two_max[:], scalar1=0.5, scalar2=0.0, op0=ALU.mult, op1=ALU.add
+        )
+        p = held.tile([P, I], F32, name="p")
+        nc.scalar.activation(out=p[:], in_=doubled[:], func=ACT.Exp, bias=neg_max[:], scale=-0.5)
         inv_norm = held.tile([P, 1], F32, name="inv_norm")
         nc.gpsimd.tensor_tensor(out=inv_norm[:], in0=sum_sq[:], in1=minus_half[:], op=ALU.pow)
 
@@ -143,7 +154,6 @@ def tile_attend_ttunitweights_kernel(tc, query, keys_words, keys_scales, dquery,
         nc.vector.tensor_scalar(
             out=shift[:], in0=sum_cross[:], scalar1=inv_norm[:], scalar2=inv_norm[:], op0=ALU.mult, op1=ALU.mult
         )
-        val_mx.append(quantize("val0", grouped0[:], P))
         w_rows = held.tile([P, I], BF16, name="w_rows", align_bytes=64)
         nc.vector.scalar_tensor_tensor(
             out=w_rows[:],
@@ -157,9 +167,10 @@ def tile_attend_ttunitweights_kernel(tc, query, keys_words, keys_scales, dquery,
         w_grouped = turn_pairs("w", w_rows, w_bank)
 
         grouped1 = gather_values(1)
+        val_mx.append(quantize("val0", grouped0[:], P, "val_pool1"))
         w_mx = quantize("w", w_grouped[:], Q)
         grouped2 = gather_values(2)
-        val_mx.append(quantize("val1", grouped1[:], P))
+        val_mx.append(quantize("val1", grouped1[:], P, "val_pool2"))
 
         early = psum.tile([P, 2, P], F32, name="early")
         for b in range(2):
@@ -170,7 +181,7 @@ def tile_attend_ttunitweights_kernel(tc, query, keys_words, keys_scales, dquery,
 
         grouped3 = gather_values(3)
         for b, grouped, drain in ((2, grouped2, nc.scalar.copy), (3, grouped3, nc.vector.tensor_copy)):
-            block_mx = quantize(f"val{b}", grouped[:], P)
+            block_mx = quantize(f"val{b}", grouped[:], P, "val_pool3" if b == 2 else None)
             late = psum.tile([P, P], F32, name=f"late{b}")
             product(late[:], w_mx, block_mx)
             late_out = held.tile([P, P], F32, name=f"late_out{b}")

@@ -36,15 +36,12 @@ def tile_attend_ttunitweights_kernel(tc, query, keys_words, keys_scales, dquery,
         val_pool = [held.tile([P, T], F32, name=f"val_pool{b}", tag=f"val_pool{b}", align_bytes=64) for b in range(BLOCKS)]
 
         nc.vector.memset(scale_pool[:].bitcast(I32), 0)
-        nc.sync.dma_start(offsets[:], offs)
-        nc.sync.dma_start(os_col[:], slot_factor.rearrange("o (p t) -> (o p) t", t=PACK))
         key_words = keys_words[0].rearrange("p n t -> p (n t)").bitcast(I32)
         nc.sync.dma_start(key_pool[:, 0 : T // 2].bitcast(I32), key_words[:, 0 : T // 2])
-        for quad in range(4):
-            nc.sync.dma_start(
-                scale_pool[32 * quad : 32 * quad + 4, :].bitcast(I32),
-                keys_scales[0, 4 * quad : 4 * quad + 4, :].bitcast(I32),
-            )
+        nc.sync.dma_start(offsets[:], offs)
+        nc.gpsimd.dma_start(os_col[:], slot_factor.rearrange("o (p t) -> (o p) t", t=PACK))
+        for r in range(4):
+            nc.sync.dma_start(scale_pool[r:P:32, :].bitcast(I32), keys_scales[0, r:16:4, :].bitcast(I32))
         nc.sync.dma_start(key_pool[:, T // 2 : T].bitcast(I32), key_words[:, T // 2 : T])
         nc.sync.dma_start(q_raw[:], query.rearrange("(p j) q -> p j q", j=PACK))
         nc.sync.dma_start(dq_raw[:], dquery.rearrange("(p j) q -> p j q", j=PACK))
@@ -75,16 +72,14 @@ def tile_attend_ttunitweights_kernel(tc, query, keys_words, keys_scales, dquery,
                 stop=True,
             )
 
-        def turn_pairs(name, rows, bank):
+        def turn_pairs(rows, bank, grouped):
             words = rows[:].bitcast(F32)
             for u in range(2):
                 nc.tensor.transpose(bank[:, u, :], words[:, u : I // 2 : 2], ident[:])
-            grouped = held.tile([P, P * PACK], BF16, name=name + "_grouped", align_bytes=64)
             nc.scalar.copy(
-                out=grouped[:].bitcast(F32).rearrange("p (c u) -> p c u", u=2),
+                out=grouped.bitcast(F32).rearrange("p (c u) -> p c u", u=2),
                 in_=bank[:].rearrange("p u c -> p c u"),
             )
-            return grouped
 
         key_scales = held.tile([P, I], U8, name="key_scales", align_bytes=64)
         nc.vector.tensor_copy(key_scales[:], scale_pool[:].indirect(offsets[:]))
@@ -118,30 +113,27 @@ def tile_attend_ttunitweights_kernel(tc, query, keys_words, keys_scales, dquery,
             out=p_sq[:], in_=doubled[:], func=ACT.Exp, bias=neg_two_max[:], scale=-1.0, accum_out=sum_sq[:]
         )
         neg_max = held.tile([P, 1], F32, name="neg_max")
-        nc.gpsimd.tensor_scalar(
-            out=neg_max[:], in0=neg_two_max[:], scalar1=0.5, scalar2=0.0, op0=ALU.mult, op1=ALU.add
-        )
-        p = held.tile([P, I], F32, name="p")
+        nc.scalar.activation(out=neg_max[:], in_=neg_two_max[:], func=ACT.Copy, scale=0.5)
+        p = held.tile([P, I], F32, name="p", tag="p", align_bytes=64)
         nc.scalar.activation(out=p[:], in_=doubled[:], func=ACT.Exp, bias=neg_max[:], scale=-0.5)
         inv_norm = held.tile([P, 1], F32, name="inv_norm")
         nc.gpsimd.tensor_tensor(out=inv_norm[:], in0=sum_sq[:], in1=minus_half[:], op=ALU.pow)
 
         val_banks = [psum.tile([P, 2, P], F32, name=f"val_bank{k}") for k in range(2)]
-        val_mx = []
+        picked = [held.tile([P, I], BF16, name=f"picked{b}", align_bytes=64) for b in range(BLOCKS)]
+        first = held.tile([P, I], BF16, name="first", align_bytes=64)
+        middle = held.tile([P, 2 * I], BF16, name="middle", align_bytes=64)
+        last = held.tile([P, I], BF16, name="last", align_bytes=64)
 
-        def gather_values(b):
-            picked = held.tile([P, I], BF16, name=f"picked{b}", align_bytes=64)
-            nc.vector.tensor_copy(picked[:], val_pool[b][:].indirect(offsets[:]))
-            return turn_pairs(f"val{b}", picked, val_banks[b % 2])
-
-        grouped0 = gather_values(0)
+        nc.vector.tensor_copy(picked[0][:], val_pool[0][:].indirect(offsets[:]))
+        turn_pairs(picked[0], val_banks[0], first[:])
 
         ta_p_sq = held.tile([P, I], F32, name="ta_p_sq")
         sum_cross = held.tile([P, 1], F32, name="sum_cross")
         nc.vector.scalar_tensor_tensor(
             out=ta_p_sq[:], in0=ta[:], scalar=1.0, in1=p_sq[:], op0=ALU.mult, op1=ALU.mult, accum_out=sum_cross[:]
         )
-        factor = held.tile([P, P, PACK], F32, name="factor")
+        factor = held.tile([P, P, PACK], F32, name="factor", tag="factor", align_bytes=64)
         nc.vector.scalar_tensor_tensor(
             out=factor[:],
             in0=p[:].rearrange("q (s t) -> q s t", t=PACK),
@@ -154,6 +146,7 @@ def tile_attend_ttunitweights_kernel(tc, query, keys_words, keys_scales, dquery,
         nc.vector.tensor_scalar(
             out=shift[:], in0=sum_cross[:], scalar1=inv_norm[:], scalar2=inv_norm[:], op0=ALU.mult, op1=ALU.mult
         )
+        first_mx = quantize("first", first[:], P, "p")
         w_rows = held.tile([P, I], BF16, name="w_rows", align_bytes=64)
         nc.vector.scalar_tensor_tensor(
             out=w_rows[:],
@@ -164,26 +157,27 @@ def tile_attend_ttunitweights_kernel(tc, query, keys_words, keys_scales, dquery,
             op1=ALU.mult,
         )
         w_bank = psum.tile([P, 2, P], F32, name="w_bank", tag="a")
-        w_grouped = turn_pairs("w", w_rows, w_bank)
+        w_grouped = held.tile([P, I], BF16, name="w_grouped", align_bytes=64)
 
-        grouped1 = gather_values(1)
-        val_mx.append(quantize("val0", grouped0[:], P, "val_pool1"))
-        w_mx = quantize("w", w_grouped[:], Q)
-        grouped2 = gather_values(2)
-        val_mx.append(quantize("val1", grouped1[:], P, "val_pool2"))
+        turn_pairs(w_rows, w_bank, w_grouped[:])
+        nc.vector.tensor_copy(picked[1][:], val_pool[1][:].indirect(offsets[:]))
+        turn_pairs(picked[1], val_banks[1], middle[:, 0:I])
+        nc.vector.tensor_copy(picked[2][:], val_pool[2][:].indirect(offsets[:]))
+        w_mx = quantize("w", w_grouped[:], Q, "val_pool2")
+        turn_pairs(picked[2], val_banks[0], middle[:, I : 2 * I])
 
-        early = psum.tile([P, 2, P], F32, name="early")
-        for b in range(2):
-            product(early[:, b, :], w_mx, val_mx[b])
-        early_out = held.tile([P, 2, P], F32, name="early_out")
-        nc.scalar.copy(out=early_out[:], in_=early[:])
-        nc.sync.dma_start(out[:, 0 : 2 * P], early_out[:].rearrange("q b e -> q (b e)"))
+        def finish(name, block_mx, start, width, drain):
+            bank = psum.tile([P, width], F32, name=name + "_bank")
+            product(bank[:], w_mx, block_mx)
+            staged = held.tile([P, width], F32, name=name + "_staged")
+            drain(out=staged[:], in_=bank[:])
+            nc.sync.dma_start(out[:, start : start + width], staged[:])
 
-        grouped3 = gather_values(3)
-        for b, grouped, drain in ((2, grouped2, nc.scalar.copy), (3, grouped3, nc.vector.tensor_copy)):
-            block_mx = quantize(f"val{b}", grouped[:], P, "val_pool3" if b == 2 else None)
-            late = psum.tile([P, P], F32, name=f"late{b}")
-            product(late[:], w_mx, block_mx)
-            late_out = held.tile([P, P], F32, name=f"late_out{b}")
-            drain(out=late_out[:], in_=late[:])
-            nc.sync.dma_start(out[:, b * P : (b + 1) * P], late_out[:])
+        finish("first", first_mx, 0, P, nc.scalar.copy)
+
+        nc.vector.tensor_copy(picked[3][:], val_pool[3][:].indirect(offsets[:]))
+        turn_pairs(picked[3], val_banks[1], last[:])
+        middle_mx = quantize("middle", middle[:], 2 * P, "val_pool3")
+        finish("middle", middle_mx, P, 2 * P, nc.scalar.copy)
+        last_mx = quantize("last", last[:], P)
+        finish("last", last_mx, 3 * P, P, nc.vector.tensor_copy)

@@ -12,12 +12,13 @@ U8 = mybir.dt.uint8
 FP8X4 = mybir.dt.float8_e4m3fn_x4
 ALU = mybir.AluOpType
 ACT = mybir.ActivationFunctionType
-AXIS = mybir.AxisListType
 
 P = 128
 PACK = 4
+QUADRANT = 32
+SCALE_ROWS = 16
 D, E, T, I, Q = 512, 512, 2048, 512, 128
-BLOCKS = E // P
+GROUPS = E // P
 FLOPS = 2 * Q * I * (2 * D + E)
 
 
@@ -33,53 +34,60 @@ def tile_attend_ttunitweights_kernel(tc, query, keys_words, keys_scales, dquery,
         q_raw = held.tile([P, PACK, Q], F32, name="q_raw")
         dq_raw = held.tile([P, PACK, Q], F32, name="dq_raw")
         os_col = held.tile([P, PACK], F32, name="os_col")
-        val_pool = [held.tile([P, T], F32, name=f"val_pool{b}", tag=f"val_pool{b}", align_bytes=64) for b in range(BLOCKS)]
+        val_pool = [
+            held.tile([P, T], F32, name=f"val_pool{g}", tag=f"val_pool{g}", align_bytes=64) for g in range(GROUPS)
+        ]
 
         nc.vector.memset(scale_pool[:].bitcast(I32), 0)
         key_words = keys_words[0].rearrange("p n t -> p (n t)").bitcast(I32)
         nc.sync.dma_start(key_pool[:, 0 : T // 2].bitcast(I32), key_words[:, 0 : T // 2])
         nc.sync.dma_start(offsets[:], offs)
         nc.gpsimd.dma_start(os_col[:], slot_factor.rearrange("o (p t) -> (o p) t", t=PACK))
-        for r in range(4):
-            nc.sync.dma_start(scale_pool[r:P:32, :].bitcast(I32), keys_scales[0, r:16:4, :].bitcast(I32))
+        for r in range(PACK):
+            nc.sync.dma_start(
+                scale_pool[r:P:QUADRANT, :].bitcast(I32), keys_scales[0, r:SCALE_ROWS:PACK, :].bitcast(I32)
+            )
         nc.sync.dma_start(key_pool[:, T // 2 : T].bitcast(I32), key_words[:, T // 2 : T])
         nc.sync.dma_start(q_raw[:], query.rearrange("(p j) q -> p j q", j=PACK))
         nc.sync.dma_start(dq_raw[:], dquery.rearrange("(p j) q -> p j q", j=PACK))
-        for b in range(BLOCKS):
-            nc.sync.dma_start(val_pool[b][:], vals[b * P : (b + 1) * P, :])
+        for g in range(GROUPS):
+            nc.sync.dma_start(val_pool[g][:], vals[g * P : (g + 1) * P, :])
 
         ident = held.tile([P, P], F32, name="ident")
         make_identity(nc, ident[:])
         minus_half = held.tile([P, 1], F32, name="minus_half")
         nc.gpsimd.memset(minus_half[:], -0.5)
-        warm = held.tile([P, 1], F32, name="warm")
-        nc.scalar.activation(out=warm[:], in_=minus_half[:], func=ACT.Exp)
 
-        def quantize(name, grouped, width, tag=None):
-            codes = held.tile([P, width], U32, name=name + "_codes", tag=tag or name + "_codes", align_bytes=64)
+        def quantize(name, grouped, width, behind=None):
+            codes = held.tile([P, width], U32, name=name + "_codes", tag=behind or name + "_codes", align_bytes=64)
             scales = held.tile([P, width], U8, name=name + "_scales", align_bytes=64)
             nc.vector.quantize_mx(out=codes[:].bitcast(FP8X4), scales=scales[:], in_=grouped)
             return codes, scales
 
-        def product(result, left, right):
+        def product(result, stationary, moving):
             nc.tensor.matmul_mx(
                 out=result,
-                lhsT=left[0][:].bitcast(FP8X4),
-                lhsT_scale=left[1][:],
-                rhs=right[0][:].bitcast(FP8X4),
-                rhs_scale=right[1][:],
+                lhsT=stationary[0][:].bitcast(FP8X4),
+                lhsT_scale=stationary[1][:],
+                rhs=moving[0][:].bitcast(FP8X4),
+                rhs_scale=moving[1][:],
                 start=True,
                 stop=True,
             )
 
-        def turn_pairs(rows, bank, grouped):
-            words = rows[:].bitcast(F32)
+        def turn_slots(rows, bank, grouped):
+            pairs = rows[:].bitcast(F32)
             for u in range(2):
-                nc.tensor.transpose(bank[:, u, :], words[:, u : I // 2 : 2], ident[:])
+                nc.tensor.transpose(bank[:, u, :], pairs[:, u : I // 2 : 2], ident[:])
             nc.scalar.copy(
                 out=grouped.bitcast(F32).rearrange("p (c u) -> p c u", u=2),
                 in_=bank[:].rearrange("p u c -> p c u"),
             )
+
+        def gather_values(g):
+            picked = held.tile([P, I], BF16, name=f"picked{g}", align_bytes=64)
+            nc.vector.tensor_copy(picked[:], val_pool[g][:].indirect(offsets[:]))
+            return picked
 
         key_scales = held.tile([P, I], U8, name="key_scales", align_bytes=64)
         nc.vector.tensor_copy(key_scales[:], scale_pool[:].indirect(offsets[:]))
@@ -88,9 +96,9 @@ def tile_attend_ttunitweights_kernel(tc, query, keys_words, keys_scales, dquery,
         keys = (key_codes, key_scales)
 
         q_grouped = held.tile([P, Q, PACK], BF16, name="q_grouped", align_bytes=64)
-        nc.scalar.copy(out=q_grouped[:], in_=q_raw[:].rearrange("p j q -> p q j"))
+        nc.scalar.activation(out=q_grouped[:], in_=q_raw[:].rearrange("p j q -> p q j"), func=ACT.Copy)
         dq_grouped = held.tile([P, Q, PACK], BF16, name="dq_grouped", align_bytes=64)
-        nc.scalar.copy(out=dq_grouped[:], in_=dq_raw[:].rearrange("p j q -> p q j"))
+        nc.scalar.activation(out=dq_grouped[:], in_=dq_raw[:].rearrange("p j q -> p q j"), func=ACT.Copy)
         q_mx = quantize("q", q_grouped[:].rearrange("p q j -> p (q j)"), Q)
         a = psum.tile([P, I], F32, name="a", tag="a")
         product(a[:], q_mx, keys)
@@ -102,41 +110,39 @@ def tile_attend_ttunitweights_kernel(tc, query, keys_words, keys_scales, dquery,
         for t in range(PACK):
             nc.tensor.transpose(os_rows[:, t, :], os_col[:, t : t + 1].to_broadcast([P, P]), ident[:])
 
-        doubled = held.tile([P, I], F32, name="doubled")
+        neg_two_a = held.tile([P, I], F32, name="neg_two_a")
         neg_two_max = held.tile([P, 1], F32, name="neg_two_max")
         nc.vector.tensor_scalar(
-            out=doubled[:], in0=a[:], scalar1=-2.0, scalar2=None, op0=ALU.mult, op1=ALU.min, accum_out=neg_two_max[:]
+            out=neg_two_a[:], in0=a[:], scalar1=-2.0, scalar2=None, op0=ALU.mult, op1=ALU.min, accum_out=neg_two_max[:]
         )
         p_sq = held.tile([P, I], F32, name="p_sq")
         sum_sq = held.tile([P, 1], F32, name="sum_sq")
         nc.scalar.activation(
-            out=p_sq[:], in_=doubled[:], func=ACT.Exp, bias=neg_two_max[:], scale=-1.0, accum_out=sum_sq[:]
+            out=p_sq[:], in_=neg_two_a[:], func=ACT.Exp, bias=neg_two_max[:], scale=-1.0, accum_out=sum_sq[:]
         )
         neg_max = held.tile([P, 1], F32, name="neg_max")
         nc.scalar.activation(out=neg_max[:], in_=neg_two_max[:], func=ACT.Copy, scale=0.5)
-        p = held.tile([P, I], F32, name="p", tag="p", align_bytes=64)
-        nc.scalar.activation(out=p[:], in_=doubled[:], func=ACT.Exp, bias=neg_max[:], scale=-0.5)
+        weights = held.tile([P, I], F32, name="weights", tag="weights", align_bytes=64)
+        nc.scalar.activation(out=weights[:], in_=neg_two_a[:], func=ACT.Exp, bias=neg_max[:], scale=-0.5)
         inv_norm = held.tile([P, 1], F32, name="inv_norm")
         nc.gpsimd.tensor_tensor(out=inv_norm[:], in0=sum_sq[:], in1=minus_half[:], op=ALU.pow)
 
         val_banks = [psum.tile([P, 2, P], F32, name=f"val_bank{k}") for k in range(2)]
-        picked = [held.tile([P, I], BF16, name=f"picked{b}", align_bytes=64) for b in range(BLOCKS)]
         first = held.tile([P, I], BF16, name="first", align_bytes=64)
         middle = held.tile([P, 2 * I], BF16, name="middle", align_bytes=64)
         last = held.tile([P, I], BF16, name="last", align_bytes=64)
 
-        nc.vector.tensor_copy(picked[0][:], val_pool[0][:].indirect(offsets[:]))
-        turn_pairs(picked[0], val_banks[0], first[:])
+        turn_slots(gather_values(0), val_banks[0], first[:])
 
         ta_p_sq = held.tile([P, I], F32, name="ta_p_sq")
         sum_cross = held.tile([P, 1], F32, name="sum_cross")
         nc.vector.scalar_tensor_tensor(
             out=ta_p_sq[:], in0=ta[:], scalar=1.0, in1=p_sq[:], op0=ALU.mult, op1=ALU.mult, accum_out=sum_cross[:]
         )
-        factor = held.tile([P, P, PACK], F32, name="factor", tag="factor", align_bytes=64)
+        factor = held.tile([P, P, PACK], F32, name="factor", align_bytes=64)
         nc.vector.scalar_tensor_tensor(
             out=factor[:],
-            in0=p[:].rearrange("q (s t) -> q s t", t=PACK),
+            in0=weights[:].rearrange("q (s t) -> q s t", t=PACK),
             scalar=inv_norm[:],
             in1=os_rows[:].rearrange("q t s -> q s t"),
             op0=ALU.mult,
@@ -146,7 +152,7 @@ def tile_attend_ttunitweights_kernel(tc, query, keys_words, keys_scales, dquery,
         nc.vector.tensor_scalar(
             out=shift[:], in0=sum_cross[:], scalar1=inv_norm[:], scalar2=inv_norm[:], op0=ALU.mult, op1=ALU.mult
         )
-        first_mx = quantize("first", first[:], P, "p")
+        first_mx = quantize("first", first[:], P, behind="weights")
         w_rows = held.tile([P, I], BF16, name="w_rows", align_bytes=64)
         nc.vector.scalar_tensor_tensor(
             out=w_rows[:],
@@ -158,26 +164,24 @@ def tile_attend_ttunitweights_kernel(tc, query, keys_words, keys_scales, dquery,
         )
         w_bank = psum.tile([P, 2, P], F32, name="w_bank", tag="a")
         w_grouped = held.tile([P, I], BF16, name="w_grouped", align_bytes=64)
+        turn_slots(w_rows, w_bank, w_grouped[:])
 
-        turn_pairs(w_rows, w_bank, w_grouped[:])
-        nc.vector.tensor_copy(picked[1][:], val_pool[1][:].indirect(offsets[:]))
-        turn_pairs(picked[1], val_banks[1], middle[:, 0:I])
-        nc.vector.tensor_copy(picked[2][:], val_pool[2][:].indirect(offsets[:]))
-        w_mx = quantize("w", w_grouped[:], Q, "val_pool2")
-        turn_pairs(picked[2], val_banks[0], middle[:, I : 2 * I])
+        turn_slots(gather_values(1), val_banks[1], middle[:, 0:I])
+        picked2 = gather_values(2)
+        w_mx = quantize("w", w_grouped[:], Q, behind="val_pool2")
+        turn_slots(picked2, val_banks[0], middle[:, I : 2 * I])
 
-        def finish(name, block_mx, start, width, drain):
+        def finish(name, values_mx, start, width, drain):
             bank = psum.tile([P, width], F32, name=name + "_bank")
-            product(bank[:], w_mx, block_mx)
+            product(bank[:], w_mx, values_mx)
             staged = held.tile([P, width], F32, name=name + "_staged")
             drain(out=staged[:], in_=bank[:])
             nc.sync.dma_start(out[:, start : start + width], staged[:])
 
         finish("first", first_mx, 0, P, nc.scalar.copy)
 
-        nc.vector.tensor_copy(picked[3][:], val_pool[3][:].indirect(offsets[:]))
-        turn_pairs(picked[3], val_banks[1], last[:])
-        middle_mx = quantize("middle", middle[:], 2 * P, "val_pool3")
+        turn_slots(gather_values(3), val_banks[1], last[:])
+        middle_mx = quantize("middle", middle[:], 2 * P, behind="val_pool3")
         finish("middle", middle_mx, P, 2 * P, nc.scalar.copy)
         last_mx = quantize("last", last[:], P)
         finish("last", last_mx, 3 * P, P, nc.vector.tensor_copy)

from contextlib import ExitStack

import concourse.mybir as mybir
from concourse.masks import make_identity

F32 = mybir.dt.float32
BF16 = mybir.dt.bfloat16
I32 = mybir.dt.int32
U32 = mybir.dt.uint32
U16 = mybir.dt.uint16
U8 = mybir.dt.uint8
FP8X4 = mybir.dt.float8_e4m3fn_x4
ALU = mybir.AluOpType
ACT = mybir.ActivationFunctionType

P = 128
PACK = 4
QUADRANT = 32
SCALE_ROWS = 16
D, E, T, I, Q = 512, 512, 2048, 512, 128
GROUPS = E // P
FLOPS = 2 * Q * I * (2 * D + E)


def tile_attend_ttunitweights_kernel(tc, query, keys_words, keys_scales, dquery, slot_factor, vals, offs, out):
    nc = tc.nc
    with ExitStack() as ctx:
        held = ctx.enter_context(tc.tile_pool(name="held", bufs=1))
        psum = ctx.enter_context(tc.psum_pool(name="psum", bufs=1))

        offsets = held.tile([P, I // 16], U16, name="offsets")
        key_pool = held.tile([P, T], U32, name="key_pool", align_bytes=64)
        scale_pool = held.tile([P, T], U8, name="scale_pool", align_bytes=64)
        q_raw = held.tile([P, PACK, Q], F32, name="q_raw")
        dq_raw = held.tile([P, PACK, Q], F32, name="dq_raw")
        os_col = held.tile([P, PACK], F32, name="os_col")
        val_pool = [
            held.tile([P, T], F32, name=f"val_pool{g}", tag=f"val_pool{g}", align_bytes=64) for g in range(GROUPS)
        ]

        nc.vector.memset(scale_pool[:].bitcast(I32), 0)
        key_words = keys_words[0].rearrange("p n t -> p (n t)").bitcast(I32)
        nc.sync.dma_start(key_pool[:, 0 : T // 2].bitcast(I32), key_words[:, 0 : T // 2])
        nc.sync.dma_start(offsets[:], offs)
        nc.gpsimd.dma_start(os_col[:], slot_factor.rearrange("o (p t) -> (o p) t", t=PACK))
        for r in range(PACK):
            nc.sync.dma_start(
                scale_pool[r:P:QUADRANT, :].bitcast(I32), keys_scales[0, r:SCALE_ROWS:PACK, :].bitcast(I32)
            )
        nc.sync.dma_start(key_pool[:, T // 2 : T].bitcast(I32), key_words[:, T // 2 : T])
        nc.sync.dma_start(q_raw[:], query.rearrange("(p j) q -> p j q", j=PACK))
        nc.sync.dma_start(dq_raw[:], dquery.rearrange("(p j) q -> p j q", j=PACK))
        for g in range(GROUPS):
            nc.sync.dma_start(val_pool[g][:], vals[g * P : (g + 1) * P, :])

        ident = held.tile([P, P], F32, name="ident")
        make_identity(nc, ident[:])
        minus_half = held.tile([P, 1], F32, name="minus_half")
        nc.gpsimd.memset(minus_half[:], -0.5)

        def quantize(name, grouped, width, behind=None):
            codes = held.tile([P, width], U32, name=name + "_codes", tag=behind or name + "_codes", align_bytes=64)
            scales = held.tile([P, width], U8, name=name + "_scales", align_bytes=64)
            nc.vector.quantize_mx(out=codes[:].bitcast(FP8X4), scales=scales[:], in_=grouped)
            return codes, scales

        def product(result, stationary, moving):
            nc.tensor.matmul_mx(
                out=result,
                lhsT=stationary[0][:].bitcast(FP8X4),
                lhsT_scale=stationary[1][:],
                rhs=moving[0][:].bitcast(FP8X4),
                rhs_scale=moving[1][:],
                start=True,
                stop=True,
            )

        def turn_slots(rows, bank, grouped):
            pairs = rows[:].bitcast(F32)
            for u in range(2):
                nc.tensor.transpose(bank[:, u, :], pairs[:, u : I // 2 : 2], ident[:])
            nc.scalar.copy(
                out=grouped.bitcast(F32).rearrange("p (c u) -> p c u", u=2),
                in_=bank[:].rearrange("p u c -> p c u"),
            )

        def gather_values(g):
            picked = held.tile([P, I], BF16, name=f"picked{g}", align_bytes=64)
            nc.vector.tensor_copy(picked[:], val_pool[g][:].indirect(offsets[:]))
            return picked

        key_scales = held.tile([P, I], U8, name="key_scales", align_bytes=64)
        nc.vector.tensor_copy(key_scales[:], scale_pool[:].indirect(offsets[:]))
        key_codes = held.tile([P, I], U32, name="key_codes", align_bytes=64)
        nc.vector.tensor_copy(key_codes[:], key_pool[:].indirect(offsets[:]))
        keys = (key_codes, key_scales)

        q_grouped = held.tile([P, Q, PACK], BF16, name="q_grouped", align_bytes=64)
        nc.scalar.activation(out=q_grouped[:], in_=q_raw[:].rearrange("p j q -> p q j"), func=ACT.Copy)
        dq_grouped = held.tile([P, Q, PACK], BF16, name="dq_grouped", align_bytes=64)
        nc.scalar.activation(out=dq_grouped[:], in_=dq_raw[:].rearrange("p j q -> p q j"), func=ACT.Copy)
        q_mx = quantize("q", q_grouped[:].rearrange("p q j -> p (q j)"), Q)
        a = psum.tile([P, I], F32, name="a", tag="a")
        product(a[:], q_mx, keys)
        dq_mx = quantize("dq", dq_grouped[:].rearrange("p q j -> p (q j)"), Q)
        ta = psum.tile([P, I], F32, name="ta")
        product(ta[:], dq_mx, keys)

        os_rows = psum.tile([P, PACK, P], F32, name="os_rows")
        for t in range(PACK):
            nc.tensor.transpose(os_rows[:, t, :], os_col[:, t : t + 1].to_broadcast([P, P]), ident[:])

        neg_two_a = held.tile([P, I], F32, name="neg_two_a")
        neg_two_max = held.tile([P, 1], F32, name="neg_two_max")
        nc.vector.tensor_scalar(
            out=neg_two_a[:], in0=a[:], scalar1=-2.0, scalar2=None, op0=ALU.mult, op1=ALU.min, accum_out=neg_two_max[:]
        )
        p_sq = held.tile([P, I], F32, name="p_sq")
        sum_sq = held.tile([P, 1], F32, name="sum_sq")
        nc.scalar.activation(
            out=p_sq[:], in_=neg_two_a[:], func=ACT.Exp, bias=neg_two_max[:], scale=-1.0, accum_out=sum_sq[:]
        )
        neg_max = held.tile([P, 1], F32, name="neg_max")
        nc.scalar.activation(out=neg_max[:], in_=neg_two_max[:], func=ACT.Copy, scale=0.5)
        weights = held.tile([P, I], F32, name="weights", tag="weights", align_bytes=64)
        nc.scalar.activation(out=weights[:], in_=neg_two_a[:], func=ACT.Exp, bias=neg_max[:], scale=-0.5)
        inv_norm = held.tile([P, 1], F32, name="inv_norm")
        nc.gpsimd.tensor_tensor(out=inv_norm[:], in0=sum_sq[:], in1=minus_half[:], op=ALU.pow)

        val_banks = [psum.tile([P, 2, P], F32, name=f"val_bank{k}") for k in range(2)]
        first = held.tile([P, I], BF16, name="first", align_bytes=64)
        middle = held.tile([P, 2 * I], BF16, name="middle", align_bytes=64)
        last = held.tile([P, I], BF16, name="last", align_bytes=64)

        turn_slots(gather_values(0), val_banks[0], first[:])

        ta_p_sq = held.tile([P, I], F32, name="ta_p_sq")
        sum_cross = held.tile([P, 1], F32, name="sum_cross")
        nc.vector.scalar_tensor_tensor(
            out=ta_p_sq[:], in0=ta[:], scalar=1.0, in1=p_sq[:], op0=ALU.mult, op1=ALU.mult, accum_out=sum_cross[:]
        )
        factor = held.tile([P, P, PACK], F32, name="factor", align_bytes=64)
        nc.vector.scalar_tensor_tensor(
            out=factor[:],
            in0=weights[:].rearrange("q (s t) -> q s t", t=PACK),
            scalar=inv_norm[:],
            in1=os_rows[:].rearrange("q t s -> q s t"),
            op0=ALU.mult,
            op1=ALU.mult,
        )
        shift = held.tile([P, 1], F32, name="shift")
        nc.vector.tensor_scalar(
            out=shift[:], in0=sum_cross[:], scalar1=inv_norm[:], scalar2=inv_norm[:], op0=ALU.mult, op1=ALU.mult
        )
        first_mx = quantize("first", first[:], P, behind="weights")
        w_rows = held.tile([P, I], BF16, name="w_rows", align_bytes=64)
        nc.vector.scalar_tensor_tensor(
            out=w_rows[:],
            in0=ta[:],
            scalar=shift[:],
            in1=factor[:].rearrange("q s t -> q (s t)"),
            op0=ALU.subtract,
            op1=ALU.mult,
        )
        w_bank = psum.tile([P, 2, P], F32, name="w_bank", tag="a")
        w_grouped = held.tile([P, I], BF16, name="w_grouped", align_bytes=64)
        turn_slots(w_rows, w_bank, w_grouped[:])

        turn_slots(gather_values(1), val_banks[1], middle[:, 0:I])
        picked2 = gather_values(2)
        w_mx = quantize("w", w_grouped[:], Q, behind="val_pool2")
        turn_slots(picked2, val_banks[0], middle[:, I : 2 * I])

        def finish(name, values_mx, start, width, drain):
            bank = psum.tile([P, width], F32, name=name + "_bank")
            product(bank[:], w_mx, values_mx)
            staged = held.tile([P, width], F32, name=name + "_staged")
            drain(out=staged[:], in_=bank[:])
            nc.sync.dma_start(out[:, start : start + width], staged[:])

        finish("first", first_mx, 0, P, nc.scalar.copy)

        turn_slots(gather_values(3), val_banks[1], last[:])
        middle_mx = quantize("middle", middle[:], 2 * P, behind="val_pool3")
        finish("middle", middle_mx, P, 2 * P, nc.scalar.copy)
        last_mx = quantize("last", last[:], P)
        finish("last", last_mx, 3 * P, P, nc.vector.tensor_copy)
